import numpy as np
import ml_dtypes


def mxq(x, axis, fmt="e4m3"):
    dtype, down = {"e4m3": (ml_dtypes.float8_e4m3fn, 7), "e5m2": (ml_dtypes.float8_e5m2, 14)}[fmt]
    v = np.moveaxis(np.asarray(x, np.float32).astype(ml_dtypes.bfloat16).astype(np.float64), axis, -1)
    blocks = v.reshape(v.shape[:-1] + (-1, 32))
    amax = np.abs(blocks).max(-1, keepdims=True)
    byte = np.maximum(np.where(amax > 0, np.frexp(amax)[1] - 1 + 127, 0) - down, 1)
    scale = np.exp2(byte - 127.0)
    codes = (blocks / scale).astype(np.float32).astype(dtype).astype(np.float64)
    return np.moveaxis((codes * scale).reshape(v.shape), -1, axis)


WIDE = False


def mx_kscale(k, group=512):
    if not WIDE:
        return np.ones(k)
    levels = np.array([10, -10, 5, -5, 0])
    if group != 512:
        return np.exp2(np.random.permutation(np.resize(levels, k // group))).repeat(group)
    if k % 512:
        return np.exp2(np.random.permutation(np.resize(levels, k // 32))).repeat(32)
    a = np.empty((k // 512, 16))
    for p in range(k // 512):
        a[p, :8] = np.random.permutation(np.resize(levels, 8))
        for g in range(8):
            far = levels[np.abs(levels - a[p, g]) >= 10]
            a[p, g + 8] = far[np.random.randint(len(far))]
    return np.exp2(a.ravel()).repeat(32)


def f64(x):
    return np.asarray(x).astype(np.float64)


def striped(idx):
    return np.tile(np.asarray(idx).reshape(-1, 16).T, (8, 1)).astype(np.uint16)


def unstriped(offs):
    return offs[:16].T.reshape(-1).astype(np.int64)


H, KV, D, NQ, N = 4, 4, 128, 512, 512


def setup_inputs():
    n = np.random.standard_normal
    s = mx_kscale(D, 0)[:, None]
    u = mx_kscale(N)
    t = np.random.uniform(0.5, 2.0, N) * u
    v = n((KV, N, 128))
    return {
        "qT": (n((H, D, NQ)) * s * (0.70 / np.sqrt(D))).astype(np.float32),
        "kT": (n((KV, D, N)) / s).astype(np.float32),
        "t": t.reshape(N, 1).astype(np.float32),
        "v": (v / t[:, None]).astype(np.float32),
        "kb": (0.5 * n((N, 1))).astype(np.float32),
        "og": n((H, NQ, 128)).astype(np.float32),
    }


def reference(qT, kT, t, v, kb, og):
    a = mxq(f64(kT), 1, "e4m3").transpose(0, 2, 1) @ mxq(f64(qT), 1, "e4m3")
    a = a + f64(kb)
    p = np.tanh(a)
    w = p * f64(t)
    y = mxq(w, 1, "e4m3").transpose(0, 2, 1) @ mxq(f64(v), 1, "e4m3")
    y = y / 16.0
    y = y / (1.0 + np.exp(-f64(og)))
    return y

@@ -1,0 +1,210 @@
+from contextlib import ExitStack
+
+import concourse.mybir as mybir
+
+H, D, NQ, N, E = 4, 128, 512, 512, 128
+FLOPS = 2 * H * N * NQ * D + 2 * H * NQ * N * E
+
+F32 = mybir.dt.float32
+BF16 = mybir.dt.bfloat16
+U32 = mybir.dt.uint32
+U8 = mybir.dt.uint8
+FP8X4 = mybir.dt.float8_e4m3fn_x4
+ACT = mybir.ActivationFunctionType
+ALU = mybir.AluOpType
+
+P = 128
+PACK = 4
+ROWS = D // PACK
+CHUNK = 128
+CHUNKS = NQ // CHUNK
+PAIR = 2
+RUN = 2
+K_VECTOR = 42
+
+
+def tile_rows_a_tanh_kb_gate_kernel(tc, qT, kT, t, v, kb, og, out):
+    nc = tc.nc
+    with ExitStack() as ctx:
+        sb = ctx.enter_context(tc.tile_pool(name="sb", bufs=1))
+        ps = ctx.enter_context(tc.psum_pool(name="ps", bufs=1))
+        ctx.enter_context(tc.manual_schedule())
+
+        def new(shape, dtype, name):
+            return sb.tile(shape, dtype, name=name, align_bytes=64)
+
+        def quantize(src, width, name):
+            codes = new([P, width], U32, name + "_codes")
+            scales = new([P, width], U8, name + "_scales")
+            nc.vector.quantize_mx(out=codes[:].bitcast(FP8X4), scales=scales[:], in_=src)
+            return codes, scales
+
+        def interleave(copy, dst, src):
+            copy(out=dst.rearrange("p (c i) j -> p c j i", i=RUN), in_=src.rearrange("p j (c i) -> p c j i", i=RUN))
+
+        k_rows = kT.rearrange("h (p j) n -> (h p) j n", j=PACK)
+        q_rows = qT.rearrange("h (p j) n -> (h p) j n", j=PACK)
+        v_rows = v.rearrange("h (p j) e -> p h j e", j=PACK)
+
+        k_raw = []
+        for u in range(2):
+            tl = new([P, PACK, N // 2], F32, "k_raw%d" % u)
+            nc.sync.dma_start(out=tl[:], in_=k_rows[:, :, u * 256:(u + 1) * 256])
+            k_raw.append(tl)
+        q_raw0 = new([P, PACK, CHUNK], F32, "q_raw0")
+        nc.sync.dma_start(out=q_raw0[:], in_=q_rows[:, :, 0:128])
+        kb_sb = new([P, PACK], F32, "kb_sb")
+        nc.sync.dma_start(out=kb_sb[:], in_=kb.rearrange("(p j) o -> p (j o)", j=PACK))
+        t_sb = new([P, PACK], F32, "t_sb")
+        nc.sync.dma_start(out=t_sb[:], in_=t.rearrange("(p j) o -> p (j o)", j=PACK))
+        q_raw1 = new([P, PACK, CHUNK], F32, "q_raw1")
+        nc.sync.dma_start(out=q_raw1[:], in_=q_rows[:, :, 128:256])
+        q_raw23 = new([P, PACK, 2 * CHUNK], F32, "q_raw23")
+        nc.sync.dma_start(out=q_raw23[:], in_=q_rows[:, :, 256:512])
+        v_raw = []
+        og_raw = []
+        for u in range(2):
+            tl = new([P, PAIR, PACK, E], F32, "v_raw%d" % u)
+            nc.sync.dma_start(out=tl[:], in_=v_rows[:, PAIR * u:PAIR * (u + 1), :, :])
+            v_raw.append(tl)
+        for c in range(CHUNKS):
+            tl = new([P, H, E], F32, "og_raw%d" % c)
+            nc.sync.dma_start(out=tl[:], in_=og[:, c * CHUNK:(c + 1) * CHUNK, :].rearrange("h m e -> m h e"))
+            og_raw.append(tl)
+
+        score = []
+        for h in range(H):
+            score.append(ps.tile([P, PACK, CHUNK], F32, name="score%d" % h))
+        y_bank = []
+        for b in range(4):
+            y_bank.append(ps.tile([P, 512], F32, name="y%d" % b))
+
+        k_bf = new([P, PACK, P, PACK], BF16, "k_bf")
+        for u in range(2):
+            dst = k_bf[:, :, 64 * u:64 * (u + 1), :].rearrange("p r s j -> p s j r")
+            src = k_raw[u][:].rearrange("p j (s r) -> p s j r", r=PACK)
+            nc.vector.tensor_copy(out=dst[:, :K_VECTOR], in_=src[:, :K_VECTOR])
+            nc.scalar.copy(out=dst[:, K_VECTOR:], in_=src[:, K_VECTOR:])
+        q_bf0 = new([P, CHUNK, PACK], BF16, "q_bf0")
+        interleave(nc.scalar.copy, q_bf0[:], q_raw0[:])
+        k_codes, k_scales = quantize(k_bf[:].rearrange("p r s j -> p (r s j)"), N, "k")
+        q_mx = {}
+        qc, qs = quantize(q_bf0[:].rearrange("p n j -> p (n j)"), CHUNK, "q0")
+        q_mx[0] = (qc[:], qs[:])
+
+        steps = CHUNKS * H // PAIR
+        p_tiles = {}
+        w_bf = {}
+        w_mx = {}
+        v_bf = {}
+        v_mx = {}
+        gate = {}
+        q_bf = {}
+
+        def scores(c, heads):
+            qc, qs = q_mx[c]
+            for r in range(PACK):
+                cols = slice(r * P, (r + 1) * P)
+                for h in heads:
+                    rows = slice(ROWS * h, ROWS * (h + 1))
+                    nc.tensor.matmul_mx(out=score[h][:, r, :], lhsT=k_codes[rows, cols].bitcast(FP8X4), lhsT_scale=k_scales[rows, cols],
+                                        rhs=qc[rows, :].bitcast(FP8X4), rhs_scale=qs[rows, :], start=True, stop=True)
+
+        def step_scores(n):
+            scores(n // 2, [PAIR * (n % 2), PAIR * (n % 2) + 1])
+
+        def tanh(n):
+            p_tile = new([P, PACK, PAIR * CHUNK], F32, "p%d" % n)
+            for g in range(PAIR):
+                h = PAIR * (n % 2) + g
+                for r in range(PACK):
+                    nc.scalar.activation(out=p_tile[:, r, g * CHUNK:(g + 1) * CHUNK], in_=score[h][:, r, :], func=ACT.Tanh, bias=kb_sb[:, r:r + 1])
+            p_tiles[n] = p_tile
+
+        def weigh(n):
+            w = new([P, PAIR * CHUNK, PACK], BF16, "w_bf%d" % n)
+            groups = PAIR * CHUNK // RUN
+            nc.vector.tensor_tensor(out=w[:].rearrange("p (c i) r -> p c r i", i=RUN),
+                                    in0=p_tiles[n][:].rearrange("p r (c i) -> p c r i", i=RUN),
+                                    in1=t_sb[:].unsqueeze(1).unsqueeze(3).to_broadcast([P, groups, PACK, RUN]), op=ALU.mult)
+            w_bf[n] = w
+
+        def quantize_w(n):
+            w_mx[n] = quantize(w_bf[n][:].rearrange("p n r -> p (n r)"), PAIR * CHUNK, "w%d" % n)
+
+        def round_v(u, copy):
+            tl = new([P, PAIR, E, PACK], BF16, "v_bf%d" % u)
+            for g in range(PAIR):
+                interleave(copy, tl[:, g], v_raw[u][:, g])
+            v_bf[u] = tl
+
+        def quantize_v(u):
+            v_mx[u] = quantize(v_bf[u][:].rearrange("p g e j -> p (g e j)"), PAIR * E, "v%d" % u)
+
+        def mix(n):
+            wc, ws = w_mx[n]
+            vc, vs = v_mx[n % 2]
+            for g in range(PAIR):
+                cols = slice(g * P, (g + 1) * P)
+                nc.tensor.matmul_mx(out=y_bank[n % 4][:, cols], lhsT=wc[:, cols].bitcast(FP8X4), lhsT_scale=ws[:, cols],
+                                    rhs=vc[:, cols].bitcast(FP8X4), rhs_scale=vs[:, cols], start=True, stop=True)
+
+        def sigmoid(c):
+            tl = new([P, H * E], F32, "gate%d" % c)
+            nc.scalar.activation(out=tl[:], in_=og_raw[c][:].rearrange("p h e -> p (h e)"), func=ACT.Sigmoid)
+            gate[c] = tl
+
+        def finish(n):
+            c, u = n // 2, n % 2
+            res = new([P, PAIR, E], F32, "res%d" % n)
+            nc.vector.scalar_tensor_tensor(out=res[:].rearrange("p g e -> p (g e)"), in0=y_bank[n % 4][:, :PAIR * E], scalar=1.0 / 16.0,
+                                           in1=gate[c][:, u * PAIR * E:(u + 1) * PAIR * E], op0=ALU.mult, op1=ALU.mult)
+            nc.sync.dma_start(out=out[PAIR * u:PAIR * (u + 1), c * CHUNK:(c + 1) * CHUNK, :].rearrange("h m e -> m h e"), in_=res[:])
+
+        scores(0, range(H))
+        q_bf1 = new([P, CHUNK, PACK], BF16, "q_bf1")
+        interleave(nc.vector.tensor_copy, q_bf1[:], q_raw1[:])
+        q_bf23 = new([P, 2 * CHUNK, PACK], BF16, "q_bf23")
+        interleave(nc.vector.tensor_copy, q_bf23[:], q_raw23[:])
+        qc, qs = quantize(q_bf1[:].rearrange("p n j -> p (n j)"), CHUNK, "q1")
+        q_mx[1] = (qc[:], qs[:])
+
+        tanh(0)
+        step_scores(2)
+        weigh(0)
+        qc, qs = quantize(q_bf23[:].rearrange("p n j -> p (n j)"), 2 * CHUNK, "q23")
+        q_mx[2] = (qc[:, :CHUNK], qs[:, :CHUNK])
+        q_mx[3] = (qc[:, CHUNK:], qs[:, CHUNK:])
+        tanh(1)
+        step_scores(3)
+        quantize_w(0)
+        weigh(1)
+        round_v(0, nc.vector.tensor_copy)
+        tanh(2)
+        step_scores(4)
+        quantize_w(1)
+        quantize_v(0)
+        mix(0)
+        round_v(1, nc.scalar.copy)
+        weigh(2)
+        sigmoid(0)
+        tanh(3)
+        step_scores(5)
+        quantize_v(1)
+        mix(1)
+        quantize_w(2)
+        mix(2)
+        finish(0)
+        for n in range(3, steps):
+            weigh(n)
+            if n + 1 < steps:
+                tanh(n + 1)
+            if n + 3 < steps:
+                step_scores(n + 3)
+            if n % 2 == 1:
+                sigmoid(n // 2)
+            finish(n - 2)
+            quantize_w(n)
+            mix(n)
+        finish(steps - 2)
+        finish(steps - 1)

@@ -20,7 +20,8 @@ CHUNK = 128
 CHUNKS = NQ // CHUNK
 PAIR = 2
 RUN = 2
-K_VECTOR = 42
+K_VECTOR = 86
+Y_BANKS = 4
 
 
 def tile_rows_a_tanh_kb_gate_kernel(tc, qT, kT, t, v, kb, og, out):
@@ -33,10 +34,16 @@ def tile_rows_a_tanh_kb_gate_kernel(tc, qT, kT, t, v, kb, og, out):
         def new(shape, dtype, name):
             return sb.tile(shape, dtype, name=name, align_bytes=64)
 
-        def quantize(src, width, name):
+        def load(queue, src, name):
+            tl = new(list(src.shape), F32, name)
+            queue.dma_start(out=tl[:], in_=src)
+            return tl
+
+        def quantize(src, name):
+            width = src.shape[1]
             codes = new([P, width], U32, name + "_codes")
             scales = new([P, width], U8, name + "_scales")
-            nc.vector.quantize_mx(out=codes[:].bitcast(FP8X4), scales=scales[:], in_=src)
+            nc.vector.quantize_mx(out=codes[:].bitcast(FP8X4), scales=scales[:], in_=src.rearrange("p n j -> p (n j)"))
             return codes, scales
 
         def interleave(copy, dst, src):
@@ -46,108 +53,107 @@ def tile_rows_a_tanh_kb_gate_kernel(tc, qT, kT, t, v, kb, og, out):
         q_rows = qT.rearrange("h (p j) n -> (h p) j n", j=PACK)
         v_rows = v.rearrange("h (p j) e -> p h j e", j=PACK)
 
-        k_raw = []
-        for u in range(2):
-            tl = new([P, PACK, N // 2], F32, "k_raw%d" % u)
-            nc.sync.dma_start(out=tl[:], in_=k_rows[:, :, u * 256:(u + 1) * 256])
-            k_raw.append(tl)
-        q_raw0 = new([P, PACK, CHUNK], F32, "q_raw0")
-        nc.sync.dma_start(out=q_raw0[:], in_=q_rows[:, :, 0:128])
-        kb_sb = new([P, PACK], F32, "kb_sb")
-        nc.sync.dma_start(out=kb_sb[:], in_=kb.rearrange("(p j) o -> p (j o)", j=PACK))
-        t_sb = new([P, PACK], F32, "t_sb")
-        nc.sync.dma_start(out=t_sb[:], in_=t.rearrange("(p j) o -> p (j o)", j=PACK))
-        q_raw1 = new([P, PACK, CHUNK], F32, "q_raw1")
-        nc.sync.dma_start(out=q_raw1[:], in_=q_rows[:, :, 128:256])
-        q_raw23 = new([P, PACK, 2 * CHUNK], F32, "q_raw23")
-        nc.sync.dma_start(out=q_raw23[:], in_=q_rows[:, :, 256:512])
-        v_raw = []
+        kb_sb = load(nc.scalar, kb.rearrange("(p j) o -> p (j o)", j=PACK), "kb_sb")
+        t_sb = load(nc.scalar, t.rearrange("(p j) o -> p (j o)", j=PACK), "t_sb")
+        k_raw = load(nc.sync, k_rows, "k_raw")
+        q_raw0 = load(nc.sync, q_rows[:, :, 0:128], "q_raw0")
+        v_raw = [load(nc.sync, v_rows[:, 0], "v_raw0")[:]]
+        q_raw1 = load(nc.sync, q_rows[:, :, 128:256], "q_raw1")
+        v_raw.append(load(nc.sync, v_rows[:, 1], "v_raw1")[:])
+        q_raw23 = load(nc.sync, q_rows[:, :, 256:512], "q_raw23")
+        v_raw23 = load(nc.sync, v_rows[:, 2:4], "v_raw23")
+        v_raw.extend([v_raw23[:, 0], v_raw23[:, 1]])
         og_raw = []
-        for u in range(2):
-            tl = new([P, PAIR, PACK, E], F32, "v_raw%d" % u)
-            nc.sync.dma_start(out=tl[:], in_=v_rows[:, PAIR * u:PAIR * (u + 1), :, :])
-            v_raw.append(tl)
         for c in range(CHUNKS):
-            tl = new([P, H, E], F32, "og_raw%d" % c)
-            nc.sync.dma_start(out=tl[:], in_=og[:, c * CHUNK:(c + 1) * CHUNK, :].rearrange("h m e -> m h e"))
-            og_raw.append(tl)
+            og_raw.append(load(nc.sync, og[:, c * CHUNK:(c + 1) * CHUNK, :].rearrange("h m e -> m h e"), "og_raw%d" % c))
 
         score = []
         for h in range(H):
             score.append(ps.tile([P, PACK, CHUNK], F32, name="score%d" % h))
         y_bank = []
-        for b in range(4):
+        for b in range(Y_BANKS):
             y_bank.append(ps.tile([P, 512], F32, name="y%d" % b))
 
-        k_bf = new([P, PACK, P, PACK], BF16, "k_bf")
-        for u in range(2):
-            dst = k_bf[:, :, 64 * u:64 * (u + 1), :].rearrange("p r s j -> p s j r")
-            src = k_raw[u][:].rearrange("p j (s r) -> p s j r", r=PACK)
-            nc.vector.tensor_copy(out=dst[:, :K_VECTOR], in_=src[:, :K_VECTOR])
-            nc.scalar.copy(out=dst[:, K_VECTOR:], in_=src[:, K_VECTOR:])
-        q_bf0 = new([P, CHUNK, PACK], BF16, "q_bf0")
-        interleave(nc.scalar.copy, q_bf0[:], q_raw0[:])
-        k_codes, k_scales = quantize(k_bf[:].rearrange("p r s j -> p (r s j)"), N, "k")
-        q_mx = {}
-        qc, qs = quantize(q_bf0[:].rearrange("p n j -> p (n j)"), CHUNK, "q0")
-        q_mx[0] = (qc[:], qs[:])
+        warm_in = new([P, 1], F32, "warm_in")
+        warm_out = new([P, 1], F32, "warm_out")
+        nc.vector.memset(warm_in[:], 0.0)
+        nc.scalar.activation(out=warm_out[:], in_=warm_in[:], func=ACT.Sigmoid)
 
-        steps = CHUNKS * H // PAIR
+        k_bf = new([P, N, PACK], BF16, "k_bf")
+        dst = k_bf[:].rearrange("p (r s) j -> p s j r", r=PACK)
+        src = k_raw[:].rearrange("p j (s r) -> p s j r", r=PACK)
+        nc.vector.tensor_copy(out=dst[:, :K_VECTOR], in_=src[:, :K_VECTOR])
+        nc.scalar.copy(out=dst[:, K_VECTOR:], in_=src[:, K_VECTOR:])
+        q_bf0 = new([P, CHUNK, PACK], BF16, "q_bf0")
+        interleave(nc.vector.tensor_copy, q_bf0[:, :64], q_raw0[:, :, :64])
+        interleave(nc.scalar.copy, q_bf0[:, 64:], q_raw0[:, :, 64:])
+        k_mx = [quantize(k_bf[:, :N // 2], "k0")]
+        q_mx = {0: quantize(q_bf0[:], "q0")}
+        k_mx.append(quantize(k_bf[:, N // 2:], "k1"))
+
+        steps = [(0, [0]), (0, [1])] + [(c, [2 * u, 2 * u + 1]) for c in range(CHUNKS) for u in range(2)][1:-1] + [(3, [2]), (3, [3])]
         p_tiles = {}
         w_bf = {}
         w_mx = {}
         v_bf = {}
         v_mx = {}
         gate = {}
-        q_bf = {}
 
         def scores(c, heads):
             qc, qs = q_mx[c]
             for r in range(PACK):
-                cols = slice(r * P, (r + 1) * P)
+                k_codes, k_scales = k_mx[r // 2]
+                cols = slice(r % 2 * P, (r % 2 + 1) * P)
                 for h in heads:
                     rows = slice(ROWS * h, ROWS * (h + 1))
                     nc.tensor.matmul_mx(out=score[h][:, r, :], lhsT=k_codes[rows, cols].bitcast(FP8X4), lhsT_scale=k_scales[rows, cols],
                                         rhs=qc[rows, :].bitcast(FP8X4), rhs_scale=qs[rows, :], start=True, stop=True)
 
-        def step_scores(n):
-            scores(n // 2, [PAIR * (n % 2), PAIR * (n % 2) + 1])
-
         def tanh(n):
-            p_tile = new([P, PACK, PAIR * CHUNK], F32, "p%d" % n)
-            for g in range(PAIR):
-                h = PAIR * (n % 2) + g
+            c, heads = steps[n]
+            p_tile = new([P, PACK, len(heads) * CHUNK], F32, "p%d" % n)
+            for g, h in enumerate(heads):
                 for r in range(PACK):
                     nc.scalar.activation(out=p_tile[:, r, g * CHUNK:(g + 1) * CHUNK], in_=score[h][:, r, :], func=ACT.Tanh, bias=kb_sb[:, r:r + 1])
             p_tiles[n] = p_tile
+            if c + 1 < CHUNKS:
+                scores(c + 1, heads)
 
         def weigh(n):
-            w = new([P, PAIR * CHUNK, PACK], BF16, "w_bf%d" % n)
-            groups = PAIR * CHUNK // RUN
+            width = len(steps[n][1]) * CHUNK
+            w = new([P, width, PACK], BF16, "w_bf%d" % n)
             nc.vector.tensor_tensor(out=w[:].rearrange("p (c i) r -> p c r i", i=RUN),
                                     in0=p_tiles[n][:].rearrange("p r (c i) -> p c r i", i=RUN),
-                                    in1=t_sb[:].unsqueeze(1).unsqueeze(3).to_broadcast([P, groups, PACK, RUN]), op=ALU.mult)
+                                    in1=t_sb[:].unsqueeze(1).unsqueeze(3).to_broadcast([P, width // RUN, PACK, RUN]), op=ALU.mult)
             w_bf[n] = w
 
         def quantize_w(n):
-            w_mx[n] = quantize(w_bf[n][:].rearrange("p n r -> p (n r)"), PAIR * CHUNK, "w%d" % n)
+            w_mx[n] = quantize(w_bf[n][:], "w%d" % n)
 
-        def round_v(u, copy):
-            tl = new([P, PAIR, E, PACK], BF16, "v_bf%d" % u)
-            for g in range(PAIR):
-                interleave(copy, tl[:, g], v_raw[u][:, g])
-            v_bf[u] = tl
+        def round_v(h, copy):
+            tl = new([P, E, PACK], BF16, "v_bf%d" % h)
+            interleave(copy, tl[:], v_raw[h])
+            v_bf[h] = tl
 
-        def quantize_v(u):
-            v_mx[u] = quantize(v_bf[u][:].rearrange("p g e j -> p (g e j)"), PAIR * E, "v%d" % u)
+        def quantize_v(h):
+            v_mx[h] = quantize(v_bf[h][:], "v%d" % h)
+
+        def weigh_split(n):
+            width = len(steps[n][1]) * CHUNK
+            rows = new([P, PACK, width], BF16, "w_rows%d" % n)
+            for r in range(PACK):
+                nc.scalar.activation(out=rows[:, r, :], in_=p_tiles[n][:, r, :], func=ACT.Copy, scale=t_sb[:, r:r + 1])
+            w = new([P, width, PACK], BF16, "w_bf%d" % n)
+            interleave(nc.vector.tensor_copy, w[:], rows[:])
+            w_bf[n] = w
 
         def mix(n):
             wc, ws = w_mx[n]
-            vc, vs = v_mx[n % 2]
-            for g in range(PAIR):
+            for g, h in enumerate(steps[n][1]):
+                vc, vs = v_mx[h]
                 cols = slice(g * P, (g + 1) * P)
-                nc.tensor.matmul_mx(out=y_bank[n % 4][:, cols], lhsT=wc[:, cols].bitcast(FP8X4), lhsT_scale=ws[:, cols],
-                                    rhs=vc[:, cols].bitcast(FP8X4), rhs_scale=vs[:, cols], start=True, stop=True)
+                nc.tensor.matmul_mx(out=y_bank[n % Y_BANKS][:, cols], lhsT=wc[:, cols].bitcast(FP8X4), lhsT_scale=ws[:, cols],
+                                    rhs=vc[:].bitcast(FP8X4), rhs_scale=vs[:], start=True, stop=True)
 
         def sigmoid(c):
             tl = new([P, H * E], F32, "gate%d" % c)
@@ -155,56 +161,89 @@ def tile_rows_a_tanh_kb_gate_kernel(tc, qT, kT, t, v, kb, og, out):
             gate[c] = tl
 
         def finish(n):
-            c, u = n // 2, n % 2
-            res = new([P, PAIR, E], F32, "res%d" % n)
-            nc.vector.scalar_tensor_tensor(out=res[:].rearrange("p g e -> p (g e)"), in0=y_bank[n % 4][:, :PAIR * E], scalar=1.0 / 16.0,
-                                           in1=gate[c][:, u * PAIR * E:(u + 1) * PAIR * E], op0=ALU.mult, op1=ALU.mult)
-            nc.sync.dma_start(out=out[PAIR * u:PAIR * (u + 1), c * CHUNK:(c + 1) * CHUNK, :].rearrange("h m e -> m h e"), in_=res[:])
+            c, heads = steps[n]
+            lo, hi = heads[0], heads[-1] + 1
+            res = new([P, hi - lo, E], F32, "res%d" % n)
+            nc.vector.scalar_tensor_tensor(out=res[:].rearrange("p g e -> p (g e)"), in0=y_bank[n % Y_BANKS][:, :(hi - lo) * E], scalar=1.0 / 16.0,
+                                           in1=gate[c][:, lo * E:hi * E], op0=ALU.mult, op1=ALU.mult)
+            nc.sync.dma_start(out=out[lo:hi, c * CHUNK:(c + 1) * CHUNK, :].rearrange("h m e -> m h e"), in_=res[:])
+
+        q_bf = {}
+
+        def round_q(c, copy):
+            tl = new([P, CHUNK, PACK], BF16, "q_bf%d" % c)
+            interleave(copy, tl[:], q_raw1[:] if c == 1 else q_raw23[:, :, (c - 2) * CHUNK:(c - 1) * CHUNK])
+            q_bf[c] = tl
+
+        def round_q23():
+            tl = new([P, 2 * CHUNK, PACK], BF16, "q_bf23")
+            interleave(nc.vector.tensor_copy, tl[:], q_raw23[:])
+            q_bf[2] = tl
+
+        def quantize_q23():
+            qc, qs = quantize(q_bf[2][:], "q23")
+            q_mx[2] = (qc[:, :CHUNK], qs[:, :CHUNK])
+            q_mx[3] = (qc[:, CHUNK:], qs[:, CHUNK:])
+
+        def quantize_q(c):
+            q_mx[c] = quantize(q_bf[c][:], "q%d" % c)
 
         scores(0, range(H))
-        q_bf1 = new([P, CHUNK, PACK], BF16, "q_bf1")
-        interleave(nc.vector.tensor_copy, q_bf1[:], q_raw1[:])
-        q_bf23 = new([P, 2 * CHUNK, PACK], BF16, "q_bf23")
-        interleave(nc.vector.tensor_copy, q_bf23[:], q_raw23[:])
-        qc, qs = quantize(q_bf1[:].rearrange("p n j -> p (n j)"), CHUNK, "q1")
-        q_mx[1] = (qc[:], qs[:])
-
-        tanh(0)
-        step_scores(2)
-        weigh(0)
-        qc, qs = quantize(q_bf23[:].rearrange("p n j -> p (n j)"), 2 * CHUNK, "q23")
-        q_mx[2] = (qc[:, :CHUNK], qs[:, :CHUNK])
-        q_mx[3] = (qc[:, CHUNK:], qs[:, CHUNK:])
-        tanh(1)
-        step_scores(3)
-        quantize_w(0)
-        weigh(1)
         round_v(0, nc.vector.tensor_copy)
-        tanh(2)
-        step_scores(4)
-        quantize_w(1)
+        round_q(1, nc.vector.tensor_copy)
         quantize_v(0)
-        mix(0)
-        round_v(1, nc.scalar.copy)
-        weigh(2)
-        sigmoid(0)
-        tanh(3)
-        step_scores(5)
+        quantize_q(1)
+        round_v(1, nc.vector.tensor_copy)
+        tanh(0)
+        weigh(0)
         quantize_v(1)
+        tanh(1)
+        weigh(1)
+        quantize_w(0)
+        mix(0)
+        tanh(2)
+        round_q23()
+        quantize_w(1)
         mix(1)
+        weigh(2)
+        quantize_q23()
+        tanh(3)
+        round_v(2, nc.scalar.copy)
         quantize_w(2)
+        round_v(3, nc.vector.tensor_copy)
+        weigh(3)
+        sigmoid(0)
+        tanh(4)
+        quantize_v(2)
+        quantize_w(3)
+        quantize_v(3)
         mix(2)
+        mix(3)
         finish(0)
-        for n in range(3, steps):
+        finish(1)
+        for n in range(4, 7):
             weigh(n)
-            if n + 1 < steps:
-                tanh(n + 1)
-            if n + 3 < steps:
-                step_scores(n + 3)
             if n % 2 == 1:
-                sigmoid(n // 2)
+                sigmoid((n - 3) // 2)
+            tanh(n + 1)
             finish(n - 2)
             quantize_w(n)
             mix(n)
-        finish(steps - 2)
-        finish(steps - 1)
+        weigh(7)
+        sigmoid(2)
+        tanh(8)
+        tanh(9)
+        finish(5)
+        quantize_w(7)
+        mix(7)
+        weigh_split(8)
+        finish(6)
+        weigh_split(9)
+        sigmoid(3)
+        quantize_w(8)
+        mix(8)
+        quantize_w(9)
+        mix(9)
+        finish(7)
+        finish(8)
+        finish(9)

from contextlib import ExitStack

import concourse.mybir as mybir

H, D, NQ, N, E = 4, 128, 512, 512, 128
FLOPS = 2 * H * N * NQ * D + 2 * H * NQ * N * E

F32 = mybir.dt.float32
BF16 = mybir.dt.bfloat16
U32 = mybir.dt.uint32
U8 = mybir.dt.uint8
FP8X4 = mybir.dt.float8_e4m3fn_x4
ACT = mybir.ActivationFunctionType
ALU = mybir.AluOpType

P = 128
PACK = 4
ROWS = D // PACK
CHUNK = 128
CHUNKS = NQ // CHUNK
PAIR = 2
RUN = 2
K_VECTOR = 86
Y_BANKS = 4


def tile_rows_a_tanh_kb_gate_kernel(tc, qT, kT, t, v, kb, og, out):
    nc = tc.nc
    with ExitStack() as ctx:
        sb = ctx.enter_context(tc.tile_pool(name="sb", bufs=1))
        ps = ctx.enter_context(tc.psum_pool(name="ps", bufs=1))
        ctx.enter_context(tc.manual_schedule())

        def new(shape, dtype, name):
            return sb.tile(shape, dtype, name=name, align_bytes=64)

        def load(queue, src, name):
            tl = new(list(src.shape), F32, name)
            queue.dma_start(out=tl[:], in_=src)
            return tl

        def quantize(src, name):
            width = src.shape[1]
            codes = new([P, width], U32, name + "_codes")
            scales = new([P, width], U8, name + "_scales")
            nc.vector.quantize_mx(out=codes[:].bitcast(FP8X4), scales=scales[:], in_=src.rearrange("p n j -> p (n j)"))
            return codes, scales

        def interleave(copy, dst, src):
            copy(out=dst.rearrange("p (c i) j -> p c j i", i=RUN), in_=src.rearrange("p j (c i) -> p c j i", i=RUN))

        k_rows = kT.rearrange("h (p j) n -> (h p) j n", j=PACK)
        q_rows = qT.rearrange("h (p j) n -> (h p) j n", j=PACK)
        v_rows = v.rearrange("h (p j) e -> p h j e", j=PACK)

        kb_sb = load(nc.scalar, kb.rearrange("(p j) o -> p (j o)", j=PACK), "kb_sb")
        t_sb = load(nc.scalar, t.rearrange("(p j) o -> p (j o)", j=PACK), "t_sb")
        k_raw = load(nc.sync, k_rows, "k_raw")
        q_raw0 = load(nc.sync, q_rows[:, :, 0:128], "q_raw0")
        v_raw = [load(nc.sync, v_rows[:, 0], "v_raw0")[:]]
        q_raw1 = load(nc.sync, q_rows[:, :, 128:256], "q_raw1")
        v_raw.append(load(nc.sync, v_rows[:, 1], "v_raw1")[:])
        q_raw23 = load(nc.sync, q_rows[:, :, 256:512], "q_raw23")
        v_raw23 = load(nc.sync, v_rows[:, 2:4], "v_raw23")
        v_raw.extend([v_raw23[:, 0], v_raw23[:, 1]])
        og_raw = []
        for c in range(CHUNKS):
            og_raw.append(load(nc.sync, og[:, c * CHUNK:(c + 1) * CHUNK, :].rearrange("h m e -> m h e"), "og_raw%d" % c))

        score = []
        for h in range(H):
            score.append(ps.tile([P, PACK, CHUNK], F32, name="score%d" % h))
        y_bank = []
        for b in range(Y_BANKS):
            y_bank.append(ps.tile([P, 512], F32, name="y%d" % b))

        warm_in = new([P, 1], F32, "warm_in")
        warm_out = new([P, 1], F32, "warm_out")
        nc.vector.memset(warm_in[:], 0.0)
        nc.scalar.activation(out=warm_out[:], in_=warm_in[:], func=ACT.Sigmoid)

        k_bf = new([P, N, PACK], BF16, "k_bf")
        dst = k_bf[:].rearrange("p (r s) j -> p s j r", r=PACK)
        src = k_raw[:].rearrange("p j (s r) -> p s j r", r=PACK)
        nc.vector.tensor_copy(out=dst[:, :K_VECTOR], in_=src[:, :K_VECTOR])
        nc.scalar.copy(out=dst[:, K_VECTOR:], in_=src[:, K_VECTOR:])
        q_bf0 = new([P, CHUNK, PACK], BF16, "q_bf0")
        interleave(nc.vector.tensor_copy, q_bf0[:, :64], q_raw0[:, :, :64])
        interleave(nc.scalar.copy, q_bf0[:, 64:], q_raw0[:, :, 64:])
        k_mx = [quantize(k_bf[:, :N // 2], "k0")]
        q_mx = {0: quantize(q_bf0[:], "q0")}
        k_mx.append(quantize(k_bf[:, N // 2:], "k1"))

        steps = [(0, [0]), (0, [1])] + [(c, [2 * u, 2 * u + 1]) for c in range(CHUNKS) for u in range(2)][1:-1] + [(3, [2]), (3, [3])]
        p_tiles = {}
        w_bf = {}
        w_mx = {}
        v_bf = {}
        v_mx = {}
        gate = {}

        def scores(c, heads):
            qc, qs = q_mx[c]
            for r in range(PACK):
                k_codes, k_scales = k_mx[r // 2]
                cols = slice(r % 2 * P, (r % 2 + 1) * P)
                for h in heads:
                    rows = slice(ROWS * h, ROWS * (h + 1))
                    nc.tensor.matmul_mx(out=score[h][:, r, :], lhsT=k_codes[rows, cols].bitcast(FP8X4), lhsT_scale=k_scales[rows, cols],
                                        rhs=qc[rows, :].bitcast(FP8X4), rhs_scale=qs[rows, :], start=True, stop=True)

        def tanh(n):
            c, heads = steps[n]
            p_tile = new([P, PACK, len(heads) * CHUNK], F32, "p%d" % n)
            for g, h in enumerate(heads):
                for r in range(PACK):
                    nc.scalar.activation(out=p_tile[:, r, g * CHUNK:(g + 1) * CHUNK], in_=score[h][:, r, :], func=ACT.Tanh, bias=kb_sb[:, r:r + 1])
            p_tiles[n] = p_tile
            if c + 1 < CHUNKS:
                scores(c + 1, heads)

        def weigh(n):
            width = len(steps[n][1]) * CHUNK
            w = new([P, width, PACK], BF16, "w_bf%d" % n)
            nc.vector.tensor_tensor(out=w[:].rearrange("p (c i) r -> p c r i", i=RUN),
                                    in0=p_tiles[n][:].rearrange("p r (c i) -> p c r i", i=RUN),
                                    in1=t_sb[:].unsqueeze(1).unsqueeze(3).to_broadcast([P, width // RUN, PACK, RUN]), op=ALU.mult)
            w_bf[n] = w

        def quantize_w(n):
            w_mx[n] = quantize(w_bf[n][:], "w%d" % n)

        def round_v(h, copy):
            tl = new([P, E, PACK], BF16, "v_bf%d" % h)
            interleave(copy, tl[:], v_raw[h])
            v_bf[h] = tl

        def quantize_v(h):
            v_mx[h] = quantize(v_bf[h][:], "v%d" % h)

        def weigh_split(n):
            width = len(steps[n][1]) * CHUNK
            rows = new([P, PACK, width], BF16, "w_rows%d" % n)
            for r in range(PACK):
                nc.scalar.activation(out=rows[:, r, :], in_=p_tiles[n][:, r, :], func=ACT.Copy, scale=t_sb[:, r:r + 1])
            w = new([P, width, PACK], BF16, "w_bf%d" % n)
            interleave(nc.vector.tensor_copy, w[:], rows[:])
            w_bf[n] = w

        def mix(n):
            wc, ws = w_mx[n]
            for g, h in enumerate(steps[n][1]):
                vc, vs = v_mx[h]
                cols = slice(g * P, (g + 1) * P)
                nc.tensor.matmul_mx(out=y_bank[n % Y_BANKS][:, cols], lhsT=wc[:, cols].bitcast(FP8X4), lhsT_scale=ws[:, cols],
                                    rhs=vc[:].bitcast(FP8X4), rhs_scale=vs[:], start=True, stop=True)

        def sigmoid(c):
            tl = new([P, H * E], F32, "gate%d" % c)
            nc.scalar.activation(out=tl[:], in_=og_raw[c][:].rearrange("p h e -> p (h e)"), func=ACT.Sigmoid)
            gate[c] = tl

        def finish(n):
            c, heads = steps[n]
            lo, hi = heads[0], heads[-1] + 1
            res = new([P, hi - lo, E], F32, "res%d" % n)
            nc.vector.scalar_tensor_tensor(out=res[:].rearrange("p g e -> p (g e)"), in0=y_bank[n % Y_BANKS][:, :(hi - lo) * E], scalar=1.0 / 16.0,
                                           in1=gate[c][:, lo * E:hi * E], op0=ALU.mult, op1=ALU.mult)
            nc.sync.dma_start(out=out[lo:hi, c * CHUNK:(c + 1) * CHUNK, :].rearrange("h m e -> m h e"), in_=res[:])

        q_bf = {}

        def round_q(c, copy):
            tl = new([P, CHUNK, PACK], BF16, "q_bf%d" % c)
            interleave(copy, tl[:], q_raw1[:] if c == 1 else q_raw23[:, :, (c - 2) * CHUNK:(c - 1) * CHUNK])
            q_bf[c] = tl

        def round_q23():
            tl = new([P, 2 * CHUNK, PACK], BF16, "q_bf23")
            interleave(nc.vector.tensor_copy, tl[:], q_raw23[:])
            q_bf[2] = tl

        def quantize_q23():
            qc, qs = quantize(q_bf[2][:], "q23")
            q_mx[2] = (qc[:, :CHUNK], qs[:, :CHUNK])
            q_mx[3] = (qc[:, CHUNK:], qs[:, CHUNK:])

        def quantize_q(c):
            q_mx[c] = quantize(q_bf[c][:], "q%d" % c)

        scores(0, range(H))
        round_v(0, nc.vector.tensor_copy)
        round_q(1, nc.vector.tensor_copy)
        quantize_v(0)
        quantize_q(1)
        round_v(1, nc.vector.tensor_copy)
        tanh(0)
        weigh(0)
        quantize_v(1)
        tanh(1)
        weigh(1)
        quantize_w(0)
        mix(0)
        tanh(2)
        round_q23()
        quantize_w(1)
        mix(1)
        weigh(2)
        quantize_q23()
        tanh(3)
        round_v(2, nc.scalar.copy)
        quantize_w(2)
        round_v(3, nc.vector.tensor_copy)
        weigh(3)
        sigmoid(0)
        tanh(4)
        quantize_v(2)
        quantize_w(3)
        quantize_v(3)
        mix(2)
        mix(3)
        finish(0)
        finish(1)
        for n in range(4, 7):
            weigh(n)
            if n % 2 == 1:
                sigmoid((n - 3) // 2)
            tanh(n + 1)
            finish(n - 2)
            quantize_w(n)
            mix(n)
        weigh(7)
        sigmoid(2)
        tanh(8)
        tanh(9)
        finish(5)
        quantize_w(7)
        mix(7)
        weigh_split(8)
        finish(6)
        weigh_split(9)
        sigmoid(3)
        quantize_w(8)
        mix(8)
        quantize_w(9)
        mix(9)
        finish(7)
        finish(8)
        finish(9)
